import numpy as np
import ml_dtypes


def mxq(x, axis, fmt="e4m3"):
    dtype, down = {"e4m3": (ml_dtypes.float8_e4m3fn, 7), "e5m2": (ml_dtypes.float8_e5m2, 14)}[fmt]
    v = np.moveaxis(np.asarray(x, np.float32).astype(ml_dtypes.bfloat16).astype(np.float64), axis, -1)
    blocks = v.reshape(v.shape[:-1] + (-1, 32))
    amax = np.abs(blocks).max(-1, keepdims=True)
    byte = np.maximum(np.where(amax > 0, np.frexp(amax)[1] - 1 + 127, 0) - down, 1)
    scale = np.exp2(byte - 127.0)
    codes = (blocks / scale).astype(np.float32).astype(dtype).astype(np.float64)
    return np.moveaxis((codes * scale).reshape(v.shape), -1, axis)


WIDE = False


def mx_kscale(k):
    if not WIDE:
        return np.ones(k)
    levels = np.array([10, -10, 5, -5, 0])
    if k % 512:
        return np.exp2(np.random.permutation(np.resize(levels, k // 32))).repeat(32)
    a = np.empty((k // 512, 16))
    for p in range(k // 512):
        a[p, :8] = np.random.permutation(np.resize(levels, 8))
        for g in range(8):
            far = levels[np.abs(levels - a[p, g]) >= 10]
            a[p, g + 8] = far[np.random.randint(len(far))]
    return np.exp2(a.ravel()).repeat(32)


def f64(x):
    return np.asarray(x).astype(np.float64)


def striped8(idx):
    return np.concatenate([x.reshape(-1, 16).T for x in idx]).astype(np.uint16)


def runs(offs, k):
    lists = np.stack([offs[16 * r : 16 * r + 16].T.reshape(-1) for r in range(8)]).astype(np.int64)
    return lists[np.arange(k) % 512 // 64]


def pack_weight(w):
    k, n = w.shape
    w = f64(np.asarray(w, np.float32).astype(ml_dtypes.bfloat16)).reshape(k // 32, 32, n)
    amax = np.abs(w).max(1)
    byte = np.clip(np.where(amax > 0, np.frexp(amax)[1] - 1 + 127 - 7, 1), 1, 254)
    scaled = (w * np.exp2(127.0 - byte)[:, None, :]).reshape(k, n).astype(np.float32)
    words = np.ascontiguousarray(scaled.reshape(k // 512, 128, 4, n).transpose(0, 1, 3, 2)).astype(ml_dtypes.float8_e4m3fn).view(np.uint8)
    return words, np.ascontiguousarray(byte.astype(np.uint8).reshape(k // 512, 16, n))


def unpack_weight(words, scales):
    g, p, n, _ = words.shape
    vals = np.ascontiguousarray(words).view(ml_dtypes.float8_e4m3fn).astype(np.float64) * np.repeat(np.exp2(scales.astype(np.float64) - 127.0), 8, axis=1)[..., None]
    return vals.transpose(0, 1, 3, 2).reshape(g * 512, n)


K, T, S, N, U = 512, 2048, 512, 512, 512


def setup_inputs():
    n = np.random.standard_normal
    s = mx_kscale(K)[:, None]
    packed_xT = pack_weight(n((K, T)) * s)
    return {
        "x_words": packed_xT[0],
        "x_scales": packed_xT[1],
        "w1": (n((K, N)) / np.sqrt(K) / s).astype(np.float32),
        "norms": np.repeat(np.random.uniform(0.5, 2.0, (8, U)), 64, axis=0).astype(np.float32),
        "offs": striped8(np.random.randint(0, T, (8, S))),
        "ncode": striped8(np.random.randint(0, U, (8, S))),
    }


def reference(x_words, x_scales, w1, norms, offs, ncode):
    xq = unpack_weight(x_words, x_scales)[np.arange(K)[:, None], runs(offs, K)]
    y = mxq(f64(w1), 0, "e4m3").T @ xq
    p = y * (f64(norms)[np.arange(N)[:, None], runs(ncode, N)])
    e = np.exp(p - p.max(axis=1, keepdims=True))
    return e / e.sum(axis=1, keepdims=True)

@@ -1,0 +1,127 @@
+from contextlib import ExitStack
+
+import concourse.mybir as mybir
+
+K, T, S, N, U = 512, 2048, 512, 512, 512
+FLOPS = 2 * K * N * S
+BYTES = K * T + K // 32 * T + 4 * K * N + 4 * 8 * U + 2 * 2 * 8 * S + 4 * N * S
+
+F32 = mybir.dt.float32
+BF16 = mybir.dt.bfloat16
+I32 = mybir.dt.int32
+U32 = mybir.dt.uint32
+U16 = mybir.dt.uint16
+U8 = mybir.dt.uint8
+FP8X4 = mybir.dt.float8_e4m3fn_x4
+ALU = mybir.AluOpType
+ACT = mybir.ActivationFunctionType
+
+P = 128
+PACK = 4
+TILES = N // P
+HALF = S // 2
+VECTOR_COLUMNS = 80
+
+
+def tile_picked_neq8_none_p_kernel(tc, x_words, x_scales, w1, norms, offs, ncode, out):
+    nc = tc.nc
+    with ExitStack() as ctx:
+        keep = ctx.enter_context(tc.tile_pool(name="keep", bufs=1))
+        psum = ctx.enter_context(tc.psum_pool(name="psum", bufs=1))
+
+        offs_sb = keep.tile([P, S // 16], U16, name="offs_sb")
+        ncode_sb = keep.tile([P, S // 16], U16, name="ncode_sb")
+        word_table = keep.tile([P, T], U32, name="word_table", align_bytes=64)
+        scale_table = keep.tile([P, T], U8, name="scale_table", align_bytes=64)
+        norm_table = keep.tile([P, U], F32, name="norm_table", align_bytes=64)
+        w_raw = keep.tile([P, PACK, N], F32, name="w_raw", align_bytes=64)
+
+        nc.vector.memset(scale_table[:].bitcast(I32), 0)
+        for r in range(2):
+            nc.scalar.dma_start(scale_table[r:P:16, :].bitcast(I32), x_scales[0][r:16:2, :].bitcast(I32))
+        nc.sync.dma_start(offs_sb[:], offs)
+        nc.sync.dma_start(ncode_sb[:], ncode)
+        nc.sync.dma_start(norm_table[:], norms.rearrange("(p t) u -> p t u", t=TILES)[:, 0, :])
+        nc.sync.dma_start(w_raw[:], w1.rearrange("(p j) n -> p j n", j=PACK))
+        nc.sync.dma_start(word_table[:].bitcast(I32), x_words[0].rearrange("p c r -> p (c r)").bitcast(I32))
+
+        picked_scales = keep.tile([P, S], U8, name="picked_scales", align_bytes=64)
+        nc.vector.tensor_copy(picked_scales[:], scale_table[:].indirect(offs_sb[:]))
+        x_plane = keep.tile([P, S], U8, name="x_plane", align_bytes=64)
+        nc.vector.tensor_copy(x_plane[:].bitcast(I32), picked_scales[:].bitcast(I32))
+        for r in range(2):
+            nc.scalar.dma_start(x_plane[2 + r : P : 32, :].bitcast(I32), picked_scales[16 + r : P : 32, :].bitcast(I32))
+
+        picked_norms = keep.tile([P, S], F32, name="picked_norms", align_bytes=64)
+        for h in range(2):
+            nc.vector.tensor_copy(
+                picked_norms[:, h * HALF : (h + 1) * HALF],
+                norm_table[:].indirect(ncode_sb[:, h * HALF // 16 : (h + 1) * HALF // 16]),
+            )
+
+        w_grouped = keep.tile([P, TILES, P, PACK], BF16, name="w_grouped", align_bytes=64)
+        src = w_raw[:].rearrange("p j (m t) -> p m j t", t=TILES)
+        dst = w_grouped[:].rearrange("p t m j -> p m j t")
+        nc.vector.tensor_copy(dst[:, :VECTOR_COLUMNS], src[:, :VECTOR_COLUMNS])
+        nc.scalar.copy(dst[:, VECTOR_COLUMNS:], src[:, VECTOR_COLUMNS:])
+        w_codes = keep.tile([P, N], U32, name="w_codes", align_bytes=64)
+        w_plane = keep.tile([P, N], U8, name="w_plane", align_bytes=64)
+        nc.vector.quantize_mx(
+            out=w_codes[:].bitcast(FP8X4),
+            scales=w_plane[:],
+            in_=w_grouped[:].rearrange("p t m j -> p (t m j)"),
+        )
+
+        picked_words = keep.tile([P, S], U32, name="picked_words", align_bytes=64)
+        for h in range(2):
+            nc.vector.tensor_copy(
+                picked_words[:, h * HALF : (h + 1) * HALF],
+                word_table[:].indirect(offs_sb[:, h * HALF // 16 : (h + 1) * HALF // 16]),
+            )
+
+        banks = [psum.tile([P, S], F32, name="bank%d" % t) for t in range(TILES)]
+        for pair in range(TILES // 2):
+            for h in range(2):
+                cols = slice(h * HALF, (h + 1) * HALF)
+                for t in (2 * pair, 2 * pair + 1):
+                    rows = slice(t * P, (t + 1) * P)
+                    nc.tensor.matmul_mx(
+                        out=banks[t][:, cols],
+                        lhsT=w_codes[:, rows].bitcast(FP8X4),
+                        lhsT_scale=w_plane[:, rows],
+                        rhs=picked_words[:, cols].bitcast(FP8X4),
+                        rhs_scale=x_plane[:, cols],
+                        start=True,
+                        stop=True,
+                    )
+
+        out_rows = out.rearrange("(p t) j -> p t j", t=TILES)
+        neg = [keep.tile([P, S], F32, name="neg%d" % t, align_bytes=64) for t in range(TILES)]
+        low = [keep.tile([P, 1], F32, name="low%d" % t) for t in range(TILES)]
+        exps = [keep.tile([P, S], F32, name="exps%d" % t, align_bytes=64) for t in range(TILES)]
+        total = [keep.tile([P, 1], F32, name="total%d" % t) for t in range(TILES)]
+        inverse = [keep.tile([P, 1], F32, name="inverse%d" % t) for t in range(TILES)]
+        result = [keep.tile([P, S], F32, name="result%d" % t, align_bytes=64) for t in range(TILES)]
+
+        def scores(t):
+            nc.vector.scalar_tensor_tensor(neg[t][:], banks[t][:], -1.0, picked_norms[:], ALU.mult, ALU.mult)
+
+        def exponentials(t):
+            nc.vector.tensor_reduce(low[t][:], neg[t][:], mybir.AxisListType.X, ALU.min)
+            nc.scalar.activation(exps[t][:], neg[t][:], ACT.Exp, bias=low[t][:], scale=-1.0, accum_out=total[t][:])
+
+        def normalise(t):
+            nc.vector.reciprocal(inverse[t][:], total[t][:])
+            if t < TILES - 1:
+                nc.gpsimd.tensor_scalar(result[t][:], exps[t][:], inverse[t][:], 1.0, ALU.mult, ALU.mult)
+            else:
+                nc.vector.tensor_scalar(result[t][:], exps[t][:], inverse[t][:], None, ALU.mult)
+            nc.sync.dma_start(out_rows[:, t, :], result[t][:])
+
+        for step in range(TILES + 2):
+            if step < TILES:
+                scores(step)
+            if 1 <= step <= TILES:
+                exponentials(step - 1)
+            if step >= 2:
+                normalise(step - 2)

@@ -20,13 +20,14 @@ P = 128
 PACK = 4
 TILES = N // P
 HALF = S // 2
-VECTOR_COLUMNS = 80
+VECTOR_COLUMNS = 72
 
 
 def tile_picked_neq8_none_p_kernel(tc, x_words, x_scales, w1, norms, offs, ncode, out):
     nc = tc.nc
     with ExitStack() as ctx:
         keep = ctx.enter_context(tc.tile_pool(name="keep", bufs=1))
+        shared = ctx.enter_context(tc.tile_pool(name="shared", bufs=1))
         psum = ctx.enter_context(tc.psum_pool(name="psum", bufs=1))
 
         offs_sb = keep.tile([P, S // 16], U16, name="offs_sb")
@@ -34,23 +35,25 @@ def tile_picked_neq8_none_p_kernel(tc, x_words, x_scales, w1, norms, offs, ncode
         word_table = keep.tile([P, T], U32, name="word_table", align_bytes=64)
         scale_table = keep.tile([P, T], U8, name="scale_table", align_bytes=64)
         norm_table = keep.tile([P, U], F32, name="norm_table", align_bytes=64)
-        w_raw = keep.tile([P, PACK, N], F32, name="w_raw", align_bytes=64)
+        w_raw = keep.tile([P, PACK * N], F32, name="w_raw", align_bytes=64)
 
-        nc.vector.memset(scale_table[:].bitcast(I32), 0)
-        for r in range(2):
-            nc.scalar.dma_start(scale_table[r:P:16, :].bitcast(I32), x_scales[0][r:16:2, :].bitcast(I32))
+        nc.gpsimd.memset(scale_table[:, : T // 2].bitcast(I32), 0)
+        nc.vector.memset(scale_table[:, T // 2 :].bitcast(I32), 0)
+        x_plane = keep.tile([P, S], U8, name="x_plane", align_bytes=64)
+        nc.vector.memset(x_plane[:].bitcast(I32), 0)
+        w_rows = w1.rearrange("(p j) n -> p (j n)", j=PACK)
         nc.sync.dma_start(offs_sb[:], offs)
         nc.sync.dma_start(ncode_sb[:], ncode)
         nc.sync.dma_start(norm_table[:], norms.rearrange("(p t) u -> p t u", t=TILES)[:, 0, :])
-        nc.sync.dma_start(w_raw[:], w1.rearrange("(p j) n -> p j n", j=PACK))
+        nc.sync.dma_start(w_raw[:, : 2 * N], w_rows[:, : 2 * N])
+        nc.sync.dma_start(scale_table[0:P:8, :].bitcast(I32), x_scales[0].bitcast(I32))
+        nc.sync.dma_start(w_raw[:, 2 * N :], w_rows[:, 2 * N :])
         nc.sync.dma_start(word_table[:].bitcast(I32), x_words[0].rearrange("p c r -> p (c r)").bitcast(I32))
 
         picked_scales = keep.tile([P, S], U8, name="picked_scales", align_bytes=64)
         nc.vector.tensor_copy(picked_scales[:], scale_table[:].indirect(offs_sb[:]))
-        x_plane = keep.tile([P, S], U8, name="x_plane", align_bytes=64)
-        nc.vector.tensor_copy(x_plane[:].bitcast(I32), picked_scales[:].bitcast(I32))
-        for r in range(2):
-            nc.scalar.dma_start(x_plane[2 + r : P : 32, :].bitcast(I32), picked_scales[16 + r : P : 32, :].bitcast(I32))
+        for r in range(4):
+            nc.sync.dma_start(x_plane[r:P:32, :].bitcast(I32), picked_scales[8 * r : P : 32, :].bitcast(I32))
 
         picked_norms = keep.tile([P, S], F32, name="picked_norms", align_bytes=64)
         for h in range(2):
@@ -59,11 +62,13 @@ def tile_picked_neq8_none_p_kernel(tc, x_words, x_scales, w1, norms, offs, ncode
                 norm_table[:].indirect(ncode_sb[:, h * HALF // 16 : (h + 1) * HALF // 16]),
             )
 
-        w_grouped = keep.tile([P, TILES, P, PACK], BF16, name="w_grouped", align_bytes=64)
-        src = w_raw[:].rearrange("p j (m t) -> p m j t", t=TILES)
+        w_grouped = shared.tile([P, TILES, P, PACK], BF16, name="w_grouped", offset=0, align_bytes=64)
         dst = w_grouped[:].rearrange("p t m j -> p m j t")
+        for h in range(2):
+            pair = w_raw[:, 2 * N * h : 2 * N * (h + 1)].rearrange("p (j m t) -> p m j t", j=2, t=TILES)
+            nc.scalar.copy(dst[:, VECTOR_COLUMNS:, 2 * h : 2 * h + 2, :], pair[:, VECTOR_COLUMNS:])
+        src = w_raw[:].rearrange("p (j m t) -> p m j t", j=PACK, t=TILES)
         nc.vector.tensor_copy(dst[:, :VECTOR_COLUMNS], src[:, :VECTOR_COLUMNS])
-        nc.scalar.copy(dst[:, VECTOR_COLUMNS:], src[:, VECTOR_COLUMNS:])
         w_codes = keep.tile([P, N], U32, name="w_codes", align_bytes=64)
         w_plane = keep.tile([P, N], U8, name="w_plane", align_bytes=64)
         nc.vector.quantize_mx(
@@ -72,39 +77,45 @@ def tile_picked_neq8_none_p_kernel(tc, x_words, x_scales, w1, norms, offs, ncode
             in_=w_grouped[:].rearrange("p t m j -> p (t m j)"),
         )
 
-        picked_words = keep.tile([P, S], U32, name="picked_words", align_bytes=64)
+        picked_words = [
+            shared.tile([P, HALF], U32, name="picked_words%d" % h, offset=4 * HALF * h, align_bytes=64) for h in range(2)
+        ]
         for h in range(2):
             nc.vector.tensor_copy(
-                picked_words[:, h * HALF : (h + 1) * HALF],
+                picked_words[h][:],
                 word_table[:].indirect(offs_sb[:, h * HALF // 16 : (h + 1) * HALF // 16]),
             )
 
-        banks = [psum.tile([P, S], F32, name="bank%d" % t) for t in range(TILES)]
-        for pair in range(TILES // 2):
-            for h in range(2):
-                cols = slice(h * HALF, (h + 1) * HALF)
-                for t in (2 * pair, 2 * pair + 1):
-                    rows = slice(t * P, (t + 1) * P)
-                    nc.tensor.matmul_mx(
-                        out=banks[t][:, cols],
-                        lhsT=w_codes[:, rows].bitcast(FP8X4),
-                        lhsT_scale=w_plane[:, rows],
-                        rhs=picked_words[:, cols].bitcast(FP8X4),
-                        rhs_scale=x_plane[:, cols],
-                        start=True,
-                        stop=True,
-                    )
-
-        out_rows = out.rearrange("(p t) j -> p t j", t=TILES)
         neg = [keep.tile([P, S], F32, name="neg%d" % t, align_bytes=64) for t in range(TILES)]
         low = [keep.tile([P, 1], F32, name="low%d" % t) for t in range(TILES)]
         exps = [keep.tile([P, S], F32, name="exps%d" % t, align_bytes=64) for t in range(TILES)]
         total = [keep.tile([P, 1], F32, name="total%d" % t) for t in range(TILES)]
         inverse = [keep.tile([P, 1], F32, name="inverse%d" % t) for t in range(TILES)]
         result = [keep.tile([P, S], F32, name="result%d" % t, align_bytes=64) for t in range(TILES)]
+        raw = keep.tile([P, S], F32, name="raw", align_bytes=64)
+        out_rows = out.rearrange("(p t) j -> p t j", t=TILES)
 
-        def scores(t):
-            nc.vector.scalar_tensor_tensor(neg[t][:], banks[t][:], -1.0, picked_norms[:], ALU.mult, ALU.mult)
+        def product(t, cols):
+            rows = slice(t * P, (t + 1) * P)
+            bank = psum.tile([P, cols.stop - cols.start], F32, name="bank%d_%d" % (t, cols.start))
+            for h in range(cols.start // HALF, cols.stop // HALF):
+                nc.tensor.matmul_mx(
+                    out=bank[:, h * HALF - cols.start : (h + 1) * HALF - cols.start],
+                    lhsT=w_codes[:, rows].bitcast(FP8X4),
+                    lhsT_scale=w_plane[:, rows],
+                    rhs=picked_words[h][:].bitcast(FP8X4),
+                    rhs_scale=x_plane[:, halves[h]],
+                    start=True,
+                    stop=True,
+                )
+            return bank
+
+        def scores(t, cols, bank):
+            nc.vector.scalar_tensor_tensor(neg[t][:, cols], bank[:], -1.0, picked_norms[:, cols], ALU.mult, ALU.mult)
+
+        def scores_off_vector(t, cols, bank):
+            nc.scalar.activation(raw[:, cols], bank[:], ACT.Copy, scale=-1.0)
+            nc.gpsimd.tensor_tensor(neg[t][:, cols], raw[:, cols], picked_norms[:, cols], ALU.mult)
 
         def exponentials(t):
             nc.vector.tensor_reduce(low[t][:], neg[t][:], mybir.AxisListType.X, ALU.min)
@@ -112,16 +123,31 @@ def tile_picked_neq8_none_p_kernel(tc, x_words, x_scales, w1, norms, offs, ncode
 
         def normalise(t):
             nc.vector.reciprocal(inverse[t][:], total[t][:])
-            if t < TILES - 1:
+            if t < 2:
                 nc.gpsimd.tensor_scalar(result[t][:], exps[t][:], inverse[t][:], 1.0, ALU.mult, ALU.mult)
-            else:
+                nc.sync.dma_start(out_rows[:, t, :], result[t][:])
+            elif t == 2:
                 nc.vector.tensor_scalar(result[t][:], exps[t][:], inverse[t][:], None, ALU.mult)
-            nc.sync.dma_start(out_rows[:, t, :], result[t][:])
+                nc.sync.dma_start(out_rows[:, t, :], result[t][:])
+            else:
+                for cols, queue in zip(halves, (nc.sync, nc.scalar)):
+                    nc.vector.tensor_scalar(result[t][:, cols], exps[t][:, cols], inverse[t][:], None, ALU.mult)
+                    queue.dma_start(out_rows[:, t, cols], result[t][:, cols])
 
-        for step in range(TILES + 2):
-            if step < TILES:
-                scores(step)
-            if 1 <= step <= TILES:
-                exponentials(step - 1)
-            if step >= 2:
-                normalise(step - 2)
+        halves = (slice(0, HALF), slice(HALF, S))
+        whole = slice(0, S)
+        for cols in halves:
+            for t in range(2):
+                scores(t, cols, product(t, cols))
+        for cols in halves:
+            scores_off_vector(2, cols, product(2, cols))
+        last_bank = product(3, whole)
+        exponentials(0)
+        exponentials(1)
+        scores(3, whole, last_bank)
+        normalise(0)
+        exponentials(2)
+        normalise(1)
+        exponentials(3)
+        normalise(2)
+        normalise(3)

@@ -92,7 +92,6 @@ def tile_picked_neq8_none_p_kernel(tc, x_words, x_scales, w1, norms, offs, ncode
         total = [keep.tile([P, 1], F32, name="total%d" % t) for t in range(TILES)]
         inverse = [keep.tile([P, 1], F32, name="inverse%d" % t) for t in range(TILES)]
         result = [keep.tile([P, S], F32, name="result%d" % t, align_bytes=64) for t in range(TILES)]
-        raw = keep.tile([P, S], F32, name="raw", align_bytes=64)
         out_rows = out.rearrange("(p t) j -> p t j", t=TILES)
 
         def product(t, cols):
@@ -113,20 +112,16 @@ def tile_picked_neq8_none_p_kernel(tc, x_words, x_scales, w1, norms, offs, ncode
         def scores(t, cols, bank):
             nc.vector.scalar_tensor_tensor(neg[t][:, cols], bank[:], -1.0, picked_norms[:, cols], ALU.mult, ALU.mult)
 
-        def scores_off_vector(t, cols, bank):
-            nc.scalar.activation(raw[:, cols], bank[:], ACT.Copy, scale=-1.0)
-            nc.gpsimd.tensor_tensor(neg[t][:, cols], raw[:, cols], picked_norms[:, cols], ALU.mult)
-
         def exponentials(t):
             nc.vector.tensor_reduce(low[t][:], neg[t][:], mybir.AxisListType.X, ALU.min)
             nc.scalar.activation(exps[t][:], neg[t][:], ACT.Exp, bias=low[t][:], scale=-1.0, accum_out=total[t][:])
 
         def normalise(t):
             nc.vector.reciprocal(inverse[t][:], total[t][:])
-            if t < 2:
-                nc.gpsimd.tensor_scalar(result[t][:], exps[t][:], inverse[t][:], 1.0, ALU.mult, ALU.mult)
+            if t == 0:
+                nc.scalar.activation(result[t][:], exps[t][:], ACT.Copy, scale=inverse[t][:])
                 nc.sync.dma_start(out_rows[:, t, :], result[t][:])
-            elif t == 2:
+            elif t < TILES - 1:
                 nc.vector.tensor_scalar(result[t][:], exps[t][:], inverse[t][:], None, ALU.mult)
                 nc.sync.dma_start(out_rows[:, t, :], result[t][:])
             else:
@@ -139,13 +134,12 @@ def tile_picked_neq8_none_p_kernel(tc, x_words, x_scales, w1, norms, offs, ncode
         for cols in halves:
             for t in range(2):
                 scores(t, cols, product(t, cols))
-        for cols in halves:
-            scores_off_vector(2, cols, product(2, cols))
-        last_bank = product(3, whole)
+        banks = [product(t, whole) for t in range(2, TILES)]
         exponentials(0)
+        scores(2, whole, banks[0])
         exponentials(1)
-        scores(3, whole, last_bank)
         normalise(0)
+        scores(3, whole, banks[1])
         exponentials(2)
         normalise(1)
         exponentials(3)

@@ -1,6 +1,7 @@
 from contextlib import ExitStack
 
 import concourse.mybir as mybir
+from concourse.masks import make_identity
 
 K, T, S, N, U = 512, 2048, 512, 512, 512
 FLOPS = 2 * K * N * S
@@ -20,7 +21,10 @@ P = 128
 PACK = 4
 TILES = N // P
 HALF = S // 2
-VECTOR_COLUMNS = 72
+RUNS = 8
+GROUP = P // RUNS
+QUAD = 4
+QUADS = P // QUAD
 
 
 def tile_picked_neq8_none_p_kernel(tc, x_words, x_scales, w1, norms, offs, ncode, out):
@@ -29,62 +33,85 @@ def tile_picked_neq8_none_p_kernel(tc, x_words, x_scales, w1, norms, offs, ncode
         keep = ctx.enter_context(tc.tile_pool(name="keep", bufs=1))
         shared = ctx.enter_context(tc.tile_pool(name="shared", bufs=1))
         psum = ctx.enter_context(tc.psum_pool(name="psum", bufs=1))
+        halves = (slice(0, HALF), slice(HALF, S))
+        lists = (slice(0, HALF // 16), slice(HALF // 16, S // 16))
 
         offs_sb = keep.tile([P, S // 16], U16, name="offs_sb")
         ncode_sb = keep.tile([P, S // 16], U16, name="ncode_sb")
         word_table = keep.tile([P, T], U32, name="word_table", align_bytes=64)
         scale_table = keep.tile([P, T], U8, name="scale_table", align_bytes=64)
         norm_table = keep.tile([P, U], F32, name="norm_table", align_bytes=64)
-        w_raw = keep.tile([P, PACK * N], F32, name="w_raw", align_bytes=64)
-
-        nc.gpsimd.memset(scale_table[:, : T // 2].bitcast(I32), 0)
-        nc.vector.memset(scale_table[:, T // 2 :].bitcast(I32), 0)
+        w_cuts = (0, N // 4, N // 2, N)
+        w_raw = [
+            shared.tile(
+                [P, PACK, w_cuts[i + 1] - w_cuts[i]], F32, name="w_raw%d" % i, offset=4096 + 16 * w_cuts[i], align_bytes=64
+            )
+            for i in range(3)
+        ]
         x_plane = keep.tile([P, S], U8, name="x_plane", align_bytes=64)
+        identity = keep.tile([P, P], F32, name="identity", align_bytes=64)
+
+        nc.vector.memset(scale_table[:].bitcast(I32), 0)
+        nc.gpsimd.memset(norm_table[:], 0.0)
         nc.vector.memset(x_plane[:].bitcast(I32), 0)
-        w_rows = w1.rearrange("(p j) n -> p (j n)", j=PACK)
+        make_identity(nc, identity[:])
+
+        w_rows = w1.rearrange("(p j) n -> p j n", j=PACK)
         nc.sync.dma_start(offs_sb[:], offs)
         nc.sync.dma_start(ncode_sb[:], ncode)
-        nc.sync.dma_start(norm_table[:], norms.rearrange("(p t) u -> p t u", t=TILES)[:, 0, :])
-        nc.sync.dma_start(w_raw[:, : 2 * N], w_rows[:, : 2 * N])
+        nc.sync.dma_start(w_raw[0][:], w_rows[:, :, w_cuts[0] : w_cuts[1]])
         nc.sync.dma_start(scale_table[0:P:8, :].bitcast(I32), x_scales[0].bitcast(I32))
-        nc.sync.dma_start(w_raw[:, 2 * N :], w_rows[:, 2 * N :])
+        nc.sync.dma_start(norm_table[0:P:GROUP, :], norms.rearrange("(r i) u -> r i u", r=RUNS)[:, 0, :])
+        for i in (1, 2):
+            nc.sync.dma_start(w_raw[i][:], w_rows[:, :, w_cuts[i] : w_cuts[i + 1]])
         nc.sync.dma_start(word_table[:].bitcast(I32), x_words[0].rearrange("p c r -> p (c r)").bitcast(I32))
 
         picked_scales = keep.tile([P, S], U8, name="picked_scales", align_bytes=64)
         nc.vector.tensor_copy(picked_scales[:], scale_table[:].indirect(offs_sb[:]))
         for r in range(4):
-            nc.sync.dma_start(x_plane[r:P:32, :].bitcast(I32), picked_scales[8 * r : P : 32, :].bitcast(I32))
+            nc.scalar.dma_start(x_plane[r:P:32, :].bitcast(I32), picked_scales[8 * r : P : 32, :].bitcast(I32))
 
         picked_norms = keep.tile([P, S], F32, name="picked_norms", align_bytes=64)
         for h in range(2):
-            nc.vector.tensor_copy(
-                picked_norms[:, h * HALF : (h + 1) * HALF],
-                norm_table[:].indirect(ncode_sb[:, h * HALF // 16 : (h + 1) * HALF // 16]),
+            nc.vector.tensor_copy(picked_norms[:, halves[h]], norm_table[:].indirect(ncode_sb[:, lists[h]]))
+
+        w_grouped = shared.tile([P, TILES, QUADS, QUAD, PACK], BF16, name="w_grouped", offset=0, align_bytes=64)
+        grouped = w_grouped[:].rearrange("p t a b j -> p t a j b")
+        for i, copy in enumerate((nc.scalar.copy, nc.scalar.copy, nc.vector.tensor_copy)):
+            copy(
+                grouped[:, :, w_cuts[i] // (TILES * QUAD) : w_cuts[i + 1] // (TILES * QUAD)],
+                w_raw[i][:].rearrange("p j (a t b) -> p t a j b", t=TILES, b=QUAD),
             )
 
-        w_grouped = shared.tile([P, TILES, P, PACK], BF16, name="w_grouped", offset=0, align_bytes=64)
-        dst = w_grouped[:].rearrange("p t m j -> p m j t")
+        row_norms = keep.tile([P, S], F32, name="row_norms", align_bytes=64)
+        spread = shared.tile([P, S // P, RUNS, GROUP], F32, name="spread", offset=4096 + 16 * w_cuts[1], align_bytes=64)
         for h in range(2):
-            pair = w_raw[:, 2 * N * h : 2 * N * (h + 1)].rearrange("p (j m t) -> p m j t", j=2, t=TILES)
-            nc.scalar.copy(dst[:, VECTOR_COLUMNS:, 2 * h : 2 * h + 2, :], pair[:, VECTOR_COLUMNS:])
-        src = w_raw[:].rearrange("p (j m t) -> p m j t", j=PACK, t=TILES)
-        nc.vector.tensor_copy(dst[:, :VECTOR_COLUMNS], src[:, :VECTOR_COLUMNS])
+            turned = psum.tile([P, 2, P], F32, name="turned", tag="late%d" % h)
+            for c in range(2):
+                nc.tensor.transpose(turned[:, c, :], picked_norms[:, (2 * h + c) * P : (2 * h + c + 1) * P], identity[:])
+            nc.scalar.copy(
+                spread[:, 2 * h : 2 * h + 2],
+                turned[:].rearrange("p c (r i) -> p c r i", r=RUNS)[:, :, :, 0:1].to_broadcast([P, 2, RUNS, GROUP]),
+            )
+        for h in range(2):
+            turned_back = psum.tile([P, 2, P], F32, name="turned_back%d" % h)
+            for c in range(2):
+                nc.tensor.transpose(turned_back[:, c, :], spread[:, 2 * h + c].rearrange("p r i -> p (r i)"), identity[:])
+            nc.scalar.copy(row_norms[:, halves[h]], turned_back[:].rearrange("p c j -> p (c j)"))
+
         w_codes = keep.tile([P, N], U32, name="w_codes", align_bytes=64)
         w_plane = keep.tile([P, N], U8, name="w_plane", align_bytes=64)
         nc.vector.quantize_mx(
             out=w_codes[:].bitcast(FP8X4),
             scales=w_plane[:],
-            in_=w_grouped[:].rearrange("p t m j -> p (t m j)"),
+            in_=w_grouped[:].rearrange("p t a b j -> p (t a b j)"),
         )
 
         picked_words = [
             shared.tile([P, HALF], U32, name="picked_words%d" % h, offset=4 * HALF * h, align_bytes=64) for h in range(2)
         ]
         for h in range(2):
-            nc.vector.tensor_copy(
-                picked_words[h][:],
-                word_table[:].indirect(offs_sb[:, h * HALF // 16 : (h + 1) * HALF // 16]),
-            )
+            nc.vector.tensor_copy(picked_words[h][:], word_table[:].indirect(offs_sb[:, lists[h]]))
 
         neg = [keep.tile([P, S], F32, name="neg%d" % t, align_bytes=64) for t in range(TILES)]
         low = [keep.tile([P, 1], F32, name="low%d" % t) for t in range(TILES)]
@@ -92,11 +119,11 @@ def tile_picked_neq8_none_p_kernel(tc, x_words, x_scales, w1, norms, offs, ncode
         total = [keep.tile([P, 1], F32, name="total%d" % t) for t in range(TILES)]
         inverse = [keep.tile([P, 1], F32, name="inverse%d" % t) for t in range(TILES)]
         result = [keep.tile([P, S], F32, name="result%d" % t, align_bytes=64) for t in range(TILES)]
-        out_rows = out.rearrange("(p t) j -> p t j", t=TILES)
+        out_rows = out.rearrange("(a t b) j -> t a b j", t=TILES, b=QUAD)
 
-        def product(t, cols):
+        def product(t, cols, tag):
             rows = slice(t * P, (t + 1) * P)
-            bank = psum.tile([P, cols.stop - cols.start], F32, name="bank%d_%d" % (t, cols.start))
+            bank = psum.tile([P, cols.stop - cols.start], F32, name="bank", tag=tag)
             for h in range(cols.start // HALF, cols.stop // HALF):
                 nc.tensor.matmul_mx(
                     out=bank[:, h * HALF - cols.start : (h + 1) * HALF - cols.start],
@@ -110,7 +137,7 @@ def tile_picked_neq8_none_p_kernel(tc, x_words, x_scales, w1, norms, offs, ncode
             return bank
 
         def scores(t, cols, bank):
-            nc.vector.scalar_tensor_tensor(neg[t][:, cols], bank[:], -1.0, picked_norms[:, cols], ALU.mult, ALU.mult)
+            nc.vector.scalar_tensor_tensor(neg[t][:, cols], bank[:], -1.0, row_norms[:, cols], ALU.mult, ALU.mult)
 
         def exponentials(t):
             nc.vector.tensor_reduce(low[t][:], neg[t][:], mybir.AxisListType.X, ALU.min)
@@ -120,28 +147,27 @@ def tile_picked_neq8_none_p_kernel(tc, x_words, x_scales, w1, norms, offs, ncode
             nc.vector.reciprocal(inverse[t][:], total[t][:])
             if t == 0:
                 nc.scalar.activation(result[t][:], exps[t][:], ACT.Copy, scale=inverse[t][:])
-                nc.sync.dma_start(out_rows[:, t, :], result[t][:])
+                nc.sync.dma_start(out_rows[t], result[t][:])
             elif t < TILES - 1:
                 nc.vector.tensor_scalar(result[t][:], exps[t][:], inverse[t][:], None, ALU.mult)
-                nc.sync.dma_start(out_rows[:, t, :], result[t][:])
+                nc.sync.dma_start(out_rows[t], result[t][:])
             else:
                 for cols, queue in zip(halves, (nc.sync, nc.scalar)):
                     nc.vector.tensor_scalar(result[t][:, cols], exps[t][:, cols], inverse[t][:], None, ALU.mult)
-                    queue.dma_start(out_rows[:, t, cols], result[t][:, cols])
+                    queue.dma_start(out_rows[t][:, :, cols], result[t][:, cols])
 
-        halves = (slice(0, HALF), slice(HALF, S))
         whole = slice(0, S)
         for cols in halves:
             for t in range(2):
-                scores(t, cols, product(t, cols))
-        banks = [product(t, whole) for t in range(2, TILES)]
+                scores(t, cols, product(t, cols, "early%d_%d" % (t, cols.start)))
+        banks = [product(t, whole, "late%d" % (t - 2)) for t in range(2, TILES)]
         exponentials(0)
         scores(2, whole, banks[0])
         exponentials(1)
         normalise(0)
         scores(3, whole, banks[1])
         exponentials(2)
-        normalise(1)
         exponentials(3)
+        normalise(1)
         normalise(2)
         normalise(3)

@@ -1,7 +1,6 @@
 from contextlib import ExitStack
 
 import concourse.mybir as mybir
-from concourse.masks import make_identity
 
 K, T, S, N, U = 512, 2048, 512, 512, 512
 FLOPS = 2 * K * N * S
@@ -21,10 +20,9 @@ P = 128
 PACK = 4
 TILES = N // P
 HALF = S // 2
-RUNS = 8
-GROUP = P // RUNS
 QUAD = 4
 QUADS = P // QUAD
+VECTOR_QUADS = 20
 
 
 def tile_picked_neq8_none_p_kernel(tc, x_words, x_scales, w1, norms, offs, ncode, out):
@@ -41,63 +39,42 @@ def tile_picked_neq8_none_p_kernel(tc, x_words, x_scales, w1, norms, offs, ncode
         word_table = keep.tile([P, T], U32, name="word_table", align_bytes=64)
         scale_table = keep.tile([P, T], U8, name="scale_table", align_bytes=64)
         norm_table = keep.tile([P, U], F32, name="norm_table", align_bytes=64)
-        w_cuts = (0, N // 4, N // 2, N)
-        w_raw = [
-            shared.tile(
-                [P, PACK, w_cuts[i + 1] - w_cuts[i]], F32, name="w_raw%d" % i, offset=4096 + 16 * w_cuts[i], align_bytes=64
-            )
-            for i in range(3)
-        ]
+        w_raw = keep.tile([P, PACK * N], F32, name="w_raw", align_bytes=64)
         x_plane = keep.tile([P, S], U8, name="x_plane", align_bytes=64)
-        identity = keep.tile([P, P], F32, name="identity", align_bytes=64)
 
-        nc.vector.memset(scale_table[:].bitcast(I32), 0)
-        nc.gpsimd.memset(norm_table[:], 0.0)
+        nc.vector.memset(scale_table[:, : T // 2].bitcast(I32), 0)
+        nc.gpsimd.memset(scale_table[:, T // 2 :].bitcast(I32), 0)
         nc.vector.memset(x_plane[:].bitcast(I32), 0)
-        make_identity(nc, identity[:])
 
-        w_rows = w1.rearrange("(p j) n -> p j n", j=PACK)
-        nc.sync.dma_start(offs_sb[:], offs)
+        w_rows = w1.rearrange("(p j) n -> p (j n)", j=PACK)
+        nc.sync.dma_start(norm_table[:], norms.rearrange("(p t) u -> p t u", t=TILES)[:, 0, :])
         nc.sync.dma_start(ncode_sb[:], ncode)
-        nc.sync.dma_start(w_raw[0][:], w_rows[:, :, w_cuts[0] : w_cuts[1]])
+        nc.sync.dma_start(offs_sb[:], offs)
         nc.sync.dma_start(scale_table[0:P:8, :].bitcast(I32), x_scales[0].bitcast(I32))
-        nc.sync.dma_start(norm_table[0:P:GROUP, :], norms.rearrange("(r i) u -> r i u", r=RUNS)[:, 0, :])
-        for i in (1, 2):
-            nc.sync.dma_start(w_raw[i][:], w_rows[:, :, w_cuts[i] : w_cuts[i + 1]])
+        for u in range(2):
+            nc.sync.dma_start(w_raw[:, 2 * N * u : 2 * N * (u + 1)], w_rows[:, 2 * N * u : 2 * N * (u + 1)])
         nc.sync.dma_start(word_table[:].bitcast(I32), x_words[0].rearrange("p c r -> p (c r)").bitcast(I32))
 
         picked_scales = keep.tile([P, S], U8, name="picked_scales", align_bytes=64)
         nc.vector.tensor_copy(picked_scales[:], scale_table[:].indirect(offs_sb[:]))
         for r in range(4):
-            nc.scalar.dma_start(x_plane[r:P:32, :].bitcast(I32), picked_scales[8 * r : P : 32, :].bitcast(I32))
+            nc.sync.dma_start(x_plane[r:P:32, :].bitcast(I32), picked_scales[8 * r : P : 32, :].bitcast(I32))
 
         picked_norms = keep.tile([P, S], F32, name="picked_norms", align_bytes=64)
         for h in range(2):
             nc.vector.tensor_copy(picked_norms[:, halves[h]], norm_table[:].indirect(ncode_sb[:, lists[h]]))
 
         w_grouped = shared.tile([P, TILES, QUADS, QUAD, PACK], BF16, name="w_grouped", offset=0, align_bytes=64)
-        grouped = w_grouped[:].rearrange("p t a b j -> p t a j b")
-        for i, copy in enumerate((nc.scalar.copy, nc.scalar.copy, nc.vector.tensor_copy)):
-            copy(
-                grouped[:, :, w_cuts[i] // (TILES * QUAD) : w_cuts[i + 1] // (TILES * QUAD)],
-                w_raw[i][:].rearrange("p j (a t b) -> p t a j b", t=TILES, b=QUAD),
-            )
-
-        row_norms = keep.tile([P, S], F32, name="row_norms", align_bytes=64)
-        spread = shared.tile([P, S // P, RUNS, GROUP], F32, name="spread", offset=4096 + 16 * w_cuts[1], align_bytes=64)
-        for h in range(2):
-            turned = psum.tile([P, 2, P], F32, name="turned", tag="late%d" % h)
-            for c in range(2):
-                nc.tensor.transpose(turned[:, c, :], picked_norms[:, (2 * h + c) * P : (2 * h + c + 1) * P], identity[:])
+        for u in range(2):
+            pair = w_raw[:, 2 * N * u : 2 * N * (u + 1)].rearrange("p (j a t b) -> p a t b j", j=2, t=TILES, b=QUAD)
             nc.scalar.copy(
-                spread[:, 2 * h : 2 * h + 2],
-                turned[:].rearrange("p c (r i) -> p c r i", r=RUNS)[:, :, :, 0:1].to_broadcast([P, 2, RUNS, GROUP]),
+                w_grouped[:].rearrange("p t a b j -> p a t b j")[:, VECTOR_QUADS:, :, :, 2 * u : 2 * u + 2],
+                pair[:, VECTOR_QUADS:],
             )
-        for h in range(2):
-            turned_back = psum.tile([P, 2, P], F32, name="turned_back%d" % h)
-            for c in range(2):
-                nc.tensor.transpose(turned_back[:, c, :], spread[:, 2 * h + c].rearrange("p r i -> p (r i)"), identity[:])
-            nc.scalar.copy(row_norms[:, halves[h]], turned_back[:].rearrange("p c j -> p (c j)"))
+        nc.vector.tensor_copy(
+            w_grouped[:].rearrange("p t a b j -> p t a j b")[:, :, :VECTOR_QUADS],
+            w_raw[:].rearrange("p (j a t b) -> p t a j b", j=PACK, t=TILES, b=QUAD)[:, :, :VECTOR_QUADS],
+        )
 
         w_codes = keep.tile([P, N], U32, name="w_codes", align_bytes=64)
         w_plane = keep.tile([P, N], U8, name="w_plane", align_bytes=64)
@@ -114,37 +91,45 @@ def tile_picked_neq8_none_p_kernel(tc, x_words, x_scales, w1, norms, offs, ncode
             nc.vector.tensor_copy(picked_words[h][:], word_table[:].indirect(offs_sb[:, lists[h]]))
 
         neg = [keep.tile([P, S], F32, name="neg%d" % t, align_bytes=64) for t in range(TILES)]
-        low = [keep.tile([P, 1], F32, name="low%d" % t) for t in range(TILES)]
+        low = [shared.tile([P, 1], F32, name="low%d" % t, offset=4096 + 64 * (t % 2), align_bytes=64) for t in range(TILES)]
         exps = [keep.tile([P, S], F32, name="exps%d" % t, align_bytes=64) for t in range(TILES)]
         total = [keep.tile([P, 1], F32, name="total%d" % t) for t in range(TILES)]
         inverse = [keep.tile([P, 1], F32, name="inverse%d" % t) for t in range(TILES)]
         result = [keep.tile([P, S], F32, name="result%d" % t, align_bytes=64) for t in range(TILES)]
         out_rows = out.rearrange("(a t b) j -> t a b j", t=TILES, b=QUAD)
 
-        def product(t, cols, tag):
+        def product(t, h):
             rows = slice(t * P, (t + 1) * P)
-            bank = psum.tile([P, cols.stop - cols.start], F32, name="bank", tag=tag)
-            for h in range(cols.start // HALF, cols.stop // HALF):
-                nc.tensor.matmul_mx(
-                    out=bank[:, h * HALF - cols.start : (h + 1) * HALF - cols.start],
-                    lhsT=w_codes[:, rows].bitcast(FP8X4),
-                    lhsT_scale=w_plane[:, rows],
-                    rhs=picked_words[h][:].bitcast(FP8X4),
-                    rhs_scale=x_plane[:, halves[h]],
-                    start=True,
-                    stop=True,
-                )
+            bank = psum.tile([P, HALF], F32, name="bank", tag="bank%d_%d" % (t, h))
+            nc.tensor.matmul_mx(
+                out=bank[:],
+                lhsT=w_codes[:, rows].bitcast(FP8X4),
+                lhsT_scale=w_plane[:, rows],
+                rhs=picked_words[h][:].bitcast(FP8X4),
+                rhs_scale=x_plane[:, halves[h]],
+                start=True,
+                stop=True,
+            )
             return bank
 
-        def scores(t, cols, bank):
-            nc.vector.scalar_tensor_tensor(neg[t][:, cols], bank[:], -1.0, row_norms[:, cols], ALU.mult, ALU.mult)
+        def scores(t, h, bank):
+            nc.vector.scalar_tensor_tensor(
+                neg[t][:, halves[h]], bank[:], -1.0, picked_norms[:, halves[h]], ALU.mult, ALU.mult
+            )
+
+        def scores_aside(t, h, bank):
+            sums = keep.tile([P, HALF], F32, name="sums%d" % t, align_bytes=64)
+            nc.scalar.activation(sums[:], bank[:], ACT.Copy, scale=-1.0)
+            nc.gpsimd.tensor_tensor(neg[t][:, halves[h]], sums[:], picked_norms[:, halves[h]], ALU.mult)
 
         def exponentials(t):
             nc.vector.tensor_reduce(low[t][:], neg[t][:], mybir.AxisListType.X, ALU.min)
             nc.scalar.activation(exps[t][:], neg[t][:], ACT.Exp, bias=low[t][:], scale=-1.0, accum_out=total[t][:])
 
-        def normalise(t):
+        def invert(t):
             nc.vector.reciprocal(inverse[t][:], total[t][:])
+
+        def normalise(t):
             if t == 0:
                 nc.scalar.activation(result[t][:], exps[t][:], ACT.Copy, scale=inverse[t][:])
                 nc.sync.dma_start(out_rows[t], result[t][:])
@@ -156,18 +141,22 @@ def tile_picked_neq8_none_p_kernel(tc, x_words, x_scales, w1, norms, offs, ncode
                     nc.vector.tensor_scalar(result[t][:, cols], exps[t][:, cols], inverse[t][:], None, ALU.mult)
                     queue.dma_start(out_rows[t][:, :, cols], result[t][:, cols])
 
-        whole = slice(0, S)
-        for cols in halves:
+        for h in range(2):
             for t in range(2):
-                scores(t, cols, product(t, cols, "early%d_%d" % (t, cols.start)))
-        banks = [product(t, whole, "late%d" % (t - 2)) for t in range(2, TILES)]
+                scores(t, h, product(t, h))
+        for t in range(2, TILES):
+            scores_aside(t, 0, product(t, 0))
+        banks = [product(t, 1) for t in range(2, TILES)]
         exponentials(0)
-        scores(2, whole, banks[0])
         exponentials(1)
+        scores(2, 1, banks[0])
+        scores(3, 1, banks[1])
+        invert(0)
         normalise(0)
-        scores(3, whole, banks[1])
         exponentials(2)
+        invert(1)
         exponentials(3)
         normalise(1)
-        normalise(2)
-        normalise(3)
+        for t in range(2, TILES):
+            invert(t)
+            normalise(t)

@@ -1,6 +1,7 @@
 from contextlib import ExitStack
 
 import concourse.mybir as mybir
+from concourse.masks import make_identity
 
 K, T, S, N, U = 512, 2048, 512, 512, 512
 FLOPS = 2 * K * N * S
@@ -22,7 +23,9 @@ TILES = N // P
 HALF = S // 2
 QUAD = 4
 QUADS = P // QUAD
-VECTOR_QUADS = 20
+RUNS = 8
+GROUP = P // RUNS
+VECTOR_QUADS = 12
 
 
 def tile_picked_neq8_none_p_kernel(tc, x_words, x_scales, w1, norms, offs, ncode, out):
@@ -39,20 +42,24 @@ def tile_picked_neq8_none_p_kernel(tc, x_words, x_scales, w1, norms, offs, ncode
         word_table = keep.tile([P, T], U32, name="word_table", align_bytes=64)
         scale_table = keep.tile([P, T], U8, name="scale_table", align_bytes=64)
         norm_table = keep.tile([P, U], F32, name="norm_table", align_bytes=64)
-        w_raw = keep.tile([P, PACK * N], F32, name="w_raw", align_bytes=64)
+        w_low = [keep.tile([P, 2, N // 2], F32, name="w_low%d" % h, align_bytes=64) for h in range(2)]
+        w_high = shared.tile([P, 2, N], F32, name="w_high", offset=8192, align_bytes=64)
         x_plane = keep.tile([P, S], U8, name="x_plane", align_bytes=64)
+        identity = keep.tile([P, P], F32, name="identity", align_bytes=64)
 
-        nc.vector.memset(scale_table[:, : T // 2].bitcast(I32), 0)
-        nc.gpsimd.memset(scale_table[:, T // 2 :].bitcast(I32), 0)
+        nc.vector.memset(scale_table[:].bitcast(I32), 0)
+        nc.vector.memset(norm_table[:], 0.0)
         nc.vector.memset(x_plane[:].bitcast(I32), 0)
+        make_identity(nc, identity[:])
 
-        w_rows = w1.rearrange("(p j) n -> p (j n)", j=PACK)
-        nc.sync.dma_start(norm_table[:], norms.rearrange("(p t) u -> p t u", t=TILES)[:, 0, :])
-        nc.sync.dma_start(ncode_sb[:], ncode)
+        w_rows = w1.rearrange("(p j) n -> p j n", j=PACK)
+        nc.sync.dma_start(w_low[0][:], w_rows[:, :2, : N // 2])
         nc.sync.dma_start(offs_sb[:], offs)
+        nc.sync.dma_start(ncode_sb[:], ncode)
         nc.sync.dma_start(scale_table[0:P:8, :].bitcast(I32), x_scales[0].bitcast(I32))
-        for u in range(2):
-            nc.sync.dma_start(w_raw[:, 2 * N * u : 2 * N * (u + 1)], w_rows[:, 2 * N * u : 2 * N * (u + 1)])
+        nc.sync.dma_start(w_low[1][:], w_rows[:, :2, N // 2 :])
+        nc.sync.dma_start(norm_table[0:P:GROUP, :], norms.rearrange("(r i) u -> r i u", r=RUNS)[:, 0, :])
+        nc.sync.dma_start(w_high[:], w_rows[:, 2:, :])
         nc.sync.dma_start(word_table[:].bitcast(I32), x_words[0].rearrange("p c r -> p (c r)").bitcast(I32))
 
         picked_scales = keep.tile([P, S], U8, name="picked_scales", align_bytes=64)
@@ -65,16 +72,31 @@ def tile_picked_neq8_none_p_kernel(tc, x_words, x_scales, w1, norms, offs, ncode
             nc.vector.tensor_copy(picked_norms[:, halves[h]], norm_table[:].indirect(ncode_sb[:, lists[h]]))
 
         w_grouped = shared.tile([P, TILES, QUADS, QUAD, PACK], BF16, name="w_grouped", offset=0, align_bytes=64)
-        for u in range(2):
-            pair = w_raw[:, 2 * N * u : 2 * N * (u + 1)].rearrange("p (j a t b) -> p a t b j", j=2, t=TILES, b=QUAD)
+        grouped = w_grouped[:].rearrange("p t a b j -> p a t b j")
+        for h in range(2):
             nc.scalar.copy(
-                w_grouped[:].rearrange("p t a b j -> p a t b j")[:, VECTOR_QUADS:, :, :, 2 * u : 2 * u + 2],
-                pair[:, VECTOR_QUADS:],
+                grouped[:, h * QUADS // 2 : (h + 1) * QUADS // 2, :, :, :2],
+                w_low[h][:].rearrange("p j (a t b) -> p a t b j", t=TILES, b=QUAD),
             )
-        nc.vector.tensor_copy(
-            w_grouped[:].rearrange("p t a b j -> p t a j b")[:, :, :VECTOR_QUADS],
-            w_raw[:].rearrange("p (j a t b) -> p t a j b", j=PACK, t=TILES, b=QUAD)[:, :, :VECTOR_QUADS],
-        )
+        high = w_high[:].rearrange("p j (a t b) -> p a t b j", t=TILES, b=QUAD)
+        nc.scalar.copy(grouped[:, VECTOR_QUADS:, :, :, 2:], high[:, VECTOR_QUADS:])
+        nc.vector.tensor_copy(grouped[:, :VECTOR_QUADS, :, :, 2:], high[:, :VECTOR_QUADS])
+
+        row_norms = keep.tile([P, S], F32, name="row_norms", align_bytes=64)
+        spread = shared.tile([P, S // P, RUNS, GROUP], F32, name="spread", offset=8192, align_bytes=64)
+        for h in range(2):
+            turned = psum.tile([P, 2, P], F32, name="turned", tag="bank%d_1" % (2 + h))
+            for c in range(2):
+                nc.tensor.transpose(turned[:, c, :], picked_norms[:, (2 * h + c) * P : (2 * h + c + 1) * P], identity[:])
+            nc.scalar.copy(
+                spread[:, 2 * h : 2 * h + 2],
+                turned[:].rearrange("p c (r i) -> p c r i", r=RUNS)[:, :, :, 0:1].to_broadcast([P, 2, RUNS, GROUP]),
+            )
+        for h in range(2):
+            turned_back = psum.tile([P, 2, P], F32, name="turned_back", tag="bank%d_0" % (2 + h))
+            for c in range(2):
+                nc.tensor.transpose(turned_back[:, c, :], spread[:, 2 * h + c].rearrange("p r i -> p (r i)"), identity[:])
+            nc.scalar.copy(row_norms[:, halves[h]], turned_back[:].rearrange("p c j -> p (c j)"))
 
         w_codes = keep.tile([P, N], U32, name="w_codes", align_bytes=64)
         w_plane = keep.tile([P, N], U8, name="w_plane", align_bytes=64)
@@ -114,13 +136,13 @@ def tile_picked_neq8_none_p_kernel(tc, x_words, x_scales, w1, norms, offs, ncode
 
         def scores(t, h, bank):
             nc.vector.scalar_tensor_tensor(
-                neg[t][:, halves[h]], bank[:], -1.0, picked_norms[:, halves[h]], ALU.mult, ALU.mult
+                neg[t][:, halves[h]], bank[:], -1.0, row_norms[:, halves[h]], ALU.mult, ALU.mult
             )
 
         def scores_aside(t, h, bank):
             sums = keep.tile([P, HALF], F32, name="sums%d" % t, align_bytes=64)
             nc.scalar.activation(sums[:], bank[:], ACT.Copy, scale=-1.0)
-            nc.gpsimd.tensor_tensor(neg[t][:, halves[h]], sums[:], picked_norms[:, halves[h]], ALU.mult)
+            nc.gpsimd.tensor_tensor(neg[t][:, halves[h]], sums[:], row_norms[:, halves[h]], ALU.mult)
 
         def exponentials(t):
             nc.vector.tensor_reduce(low[t][:], neg[t][:], mybir.AxisListType.X, ALU.min)

@@ -43,33 +43,33 @@ def tile_picked_neq8_none_p_kernel(tc, x_words, x_scales, w1, norms, offs, ncode
         scale_table = keep.tile([P, T], U8, name="scale_table", align_bytes=64)
         norm_table = keep.tile([P, U], F32, name="norm_table", align_bytes=64)
         w_low = [keep.tile([P, 2, N // 2], F32, name="w_low%d" % h, align_bytes=64) for h in range(2)]
-        w_high = shared.tile([P, 2, N], F32, name="w_high", offset=8192, align_bytes=64)
+        w_high = keep.tile([P, 2, N], F32, name="w_high", align_bytes=64)
         x_plane = keep.tile([P, S], U8, name="x_plane", align_bytes=64)
         identity = keep.tile([P, P], F32, name="identity", align_bytes=64)
 
-        nc.vector.memset(scale_table[:].bitcast(I32), 0)
         nc.vector.memset(norm_table[:], 0.0)
+        nc.vector.memset(scale_table[:].bitcast(I32), 0)
         nc.vector.memset(x_plane[:].bitcast(I32), 0)
         make_identity(nc, identity[:])
 
         w_rows = w1.rearrange("(p j) n -> p j n", j=PACK)
         nc.sync.dma_start(w_low[0][:], w_rows[:, :2, : N // 2])
-        nc.sync.dma_start(offs_sb[:], offs)
         nc.sync.dma_start(ncode_sb[:], ncode)
-        nc.sync.dma_start(scale_table[0:P:8, :].bitcast(I32), x_scales[0].bitcast(I32))
-        nc.sync.dma_start(w_low[1][:], w_rows[:, :2, N // 2 :])
+        nc.sync.dma_start(offs_sb[:], offs)
         nc.sync.dma_start(norm_table[0:P:GROUP, :], norms.rearrange("(r i) u -> r i u", r=RUNS)[:, 0, :])
+        nc.sync.dma_start(w_low[1][:], w_rows[:, :2, N // 2 :])
+        nc.sync.dma_start(scale_table[0:P:8, :].bitcast(I32), x_scales[0].bitcast(I32))
         nc.sync.dma_start(w_high[:], w_rows[:, 2:, :])
         nc.sync.dma_start(word_table[:].bitcast(I32), x_words[0].rearrange("p c r -> p (c r)").bitcast(I32))
+
+        picked_norms = keep.tile([P, S], F32, name="picked_norms", align_bytes=64)
+        for h in range(2):
+            nc.vector.tensor_copy(picked_norms[:, halves[h]], norm_table[:].indirect(ncode_sb[:, lists[h]]))
 
         picked_scales = keep.tile([P, S], U8, name="picked_scales", align_bytes=64)
         nc.vector.tensor_copy(picked_scales[:], scale_table[:].indirect(offs_sb[:]))
         for r in range(4):
             nc.sync.dma_start(x_plane[r:P:32, :].bitcast(I32), picked_scales[8 * r : P : 32, :].bitcast(I32))
-
-        picked_norms = keep.tile([P, S], F32, name="picked_norms", align_bytes=64)
-        for h in range(2):
-            nc.vector.tensor_copy(picked_norms[:, halves[h]], norm_table[:].indirect(ncode_sb[:, lists[h]]))
 
         w_grouped = shared.tile([P, TILES, QUADS, QUAD, PACK], BF16, name="w_grouped", offset=0, align_bytes=64)
         grouped = w_grouped[:].rearrange("p t a b j -> p a t b j")
@@ -83,7 +83,7 @@ def tile_picked_neq8_none_p_kernel(tc, x_words, x_scales, w1, norms, offs, ncode
         nc.vector.tensor_copy(grouped[:, :VECTOR_QUADS, :, :, 2:], high[:, :VECTOR_QUADS])
 
         row_norms = keep.tile([P, S], F32, name="row_norms", align_bytes=64)
-        spread = shared.tile([P, S // P, RUNS, GROUP], F32, name="spread", offset=8192, align_bytes=64)
+        spread = keep.tile([P, S // P, RUNS, GROUP], F32, name="spread", align_bytes=64)
         for h in range(2):
             turned = psum.tile([P, 2, P], F32, name="turned", tag="bank%d_1" % (2 + h))
             for c in range(2):

@@ -25,7 +25,7 @@ QUAD = 4
 QUADS = P // QUAD
 RUNS = 8
 GROUP = P // RUNS
-VECTOR_QUADS = 12
+VECTOR_QUADS = 16
 
 
 def tile_picked_neq8_none_p_kernel(tc, x_words, x_scales, w1, norms, offs, ncode, out):
@@ -43,7 +43,7 @@ def tile_picked_neq8_none_p_kernel(tc, x_words, x_scales, w1, norms, offs, ncode
         scale_table = keep.tile([P, T], U8, name="scale_table", align_bytes=64)
         norm_table = keep.tile([P, U], F32, name="norm_table", align_bytes=64)
         w_low = [keep.tile([P, 2, N // 2], F32, name="w_low%d" % h, align_bytes=64) for h in range(2)]
-        w_high = keep.tile([P, 2, N], F32, name="w_high", align_bytes=64)
+        w_high = shared.tile([P, 2, N], F32, name="w_high", offset=8192, align_bytes=64)
         x_plane = keep.tile([P, S], U8, name="x_plane", align_bytes=64)
         identity = keep.tile([P, P], F32, name="identity", align_bytes=64)
 
@@ -62,9 +62,8 @@ def tile_picked_neq8_none_p_kernel(tc, x_words, x_scales, w1, norms, offs, ncode
         nc.sync.dma_start(w_high[:], w_rows[:, 2:, :])
         nc.sync.dma_start(word_table[:].bitcast(I32), x_words[0].rearrange("p c r -> p (c r)").bitcast(I32))
 
-        picked_norms = keep.tile([P, S], F32, name="picked_norms", align_bytes=64)
-        for h in range(2):
-            nc.vector.tensor_copy(picked_norms[:, halves[h]], norm_table[:].indirect(ncode_sb[:, lists[h]]))
+        picked_norms = [keep.tile([P, HALF], F32, name="picked_norms%d" % h, align_bytes=64) for h in range(2)]
+        nc.vector.tensor_copy(picked_norms[0][:], norm_table[:].indirect(ncode_sb[:, lists[0]]))
 
         picked_scales = keep.tile([P, S], U8, name="picked_scales", align_bytes=64)
         nc.vector.tensor_copy(picked_scales[:], scale_table[:].indirect(offs_sb[:]))
@@ -78,16 +77,18 @@ def tile_picked_neq8_none_p_kernel(tc, x_words, x_scales, w1, norms, offs, ncode
                 grouped[:, h * QUADS // 2 : (h + 1) * QUADS // 2, :, :, :2],
                 w_low[h][:].rearrange("p j (a t b) -> p a t b j", t=TILES, b=QUAD),
             )
+            if h == 0:
+                nc.scalar.activation(picked_norms[1][:], norm_table[:].indirect(ncode_sb[:, lists[1]]), ACT.Copy)
         high = w_high[:].rearrange("p j (a t b) -> p a t b j", t=TILES, b=QUAD)
         nc.scalar.copy(grouped[:, VECTOR_QUADS:, :, :, 2:], high[:, VECTOR_QUADS:])
         nc.vector.tensor_copy(grouped[:, :VECTOR_QUADS, :, :, 2:], high[:, :VECTOR_QUADS])
 
         row_norms = keep.tile([P, S], F32, name="row_norms", align_bytes=64)
-        spread = keep.tile([P, S // P, RUNS, GROUP], F32, name="spread", align_bytes=64)
+        spread = shared.tile([P, S // P, RUNS, GROUP], F32, name="spread", offset=8192, align_bytes=64)
         for h in range(2):
             turned = psum.tile([P, 2, P], F32, name="turned", tag="bank%d_1" % (2 + h))
             for c in range(2):
-                nc.tensor.transpose(turned[:, c, :], picked_norms[:, (2 * h + c) * P : (2 * h + c + 1) * P], identity[:])
+                nc.tensor.transpose(turned[:, c, :], picked_norms[h][:, c * P : (c + 1) * P], identity[:])
             nc.scalar.copy(
                 spread[:, 2 * h : 2 * h + 2],
                 turned[:].rearrange("p c (r i) -> p c r i", r=RUNS)[:, :, :, 0:1].to_broadcast([P, 2, RUNS, GROUP]),

from contextlib import ExitStack

import concourse.mybir as mybir
from concourse.masks import make_identity

K, T, S, N, U = 512, 2048, 512, 512, 512
FLOPS = 2 * K * N * S
BYTES = K * T + K // 32 * T + 4 * K * N + 4 * 8 * U + 2 * 2 * 8 * S + 4 * N * S

F32 = mybir.dt.float32
BF16 = mybir.dt.bfloat16
I32 = mybir.dt.int32
U32 = mybir.dt.uint32
U16 = mybir.dt.uint16
U8 = mybir.dt.uint8
FP8X4 = mybir.dt.float8_e4m3fn_x4
ALU = mybir.AluOpType
ACT = mybir.ActivationFunctionType

P = 128
PACK = 4
TILES = N // P
HALF = S // 2
QUAD = 4
QUADS = P // QUAD
RUNS = 8
GROUP = P // RUNS
VECTOR_QUADS = 16


def tile_picked_neq8_none_p_kernel(tc, x_words, x_scales, w1, norms, offs, ncode, out):
    nc = tc.nc
    with ExitStack() as ctx:
        keep = ctx.enter_context(tc.tile_pool(name="keep", bufs=1))
        shared = ctx.enter_context(tc.tile_pool(name="shared", bufs=1))
        psum = ctx.enter_context(tc.psum_pool(name="psum", bufs=1))
        halves = (slice(0, HALF), slice(HALF, S))
        lists = (slice(0, HALF // 16), slice(HALF // 16, S // 16))

        offs_sb = keep.tile([P, S // 16], U16, name="offs_sb")
        ncode_sb = keep.tile([P, S // 16], U16, name="ncode_sb")
        word_table = keep.tile([P, T], U32, name="word_table", align_bytes=64)
        scale_table = keep.tile([P, T], U8, name="scale_table", align_bytes=64)
        norm_table = keep.tile([P, U], F32, name="norm_table", align_bytes=64)
        w_low = [keep.tile([P, 2, N // 2], F32, name="w_low%d" % h, align_bytes=64) for h in range(2)]
        w_high = shared.tile([P, 2, N], F32, name="w_high", offset=8192, align_bytes=64)
        x_plane = keep.tile([P, S], U8, name="x_plane", align_bytes=64)
        identity = keep.tile([P, P], F32, name="identity", align_bytes=64)

        nc.vector.memset(norm_table[:], 0.0)
        nc.vector.memset(scale_table[:].bitcast(I32), 0)
        nc.vector.memset(x_plane[:].bitcast(I32), 0)
        make_identity(nc, identity[:])

        w_rows = w1.rearrange("(p j) n -> p j n", j=PACK)
        nc.sync.dma_start(w_low[0][:], w_rows[:, :2, : N // 2])
        nc.sync.dma_start(ncode_sb[:], ncode)
        nc.sync.dma_start(offs_sb[:], offs)
        nc.sync.dma_start(norm_table[0:P:GROUP, :], norms.rearrange("(r i) u -> r i u", r=RUNS)[:, 0, :])
        nc.sync.dma_start(w_low[1][:], w_rows[:, :2, N // 2 :])
        nc.sync.dma_start(scale_table[0:P:8, :].bitcast(I32), x_scales[0].bitcast(I32))
        nc.sync.dma_start(w_high[:], w_rows[:, 2:, :])
        nc.sync.dma_start(word_table[:].bitcast(I32), x_words[0].rearrange("p c r -> p (c r)").bitcast(I32))

        picked_norms = [keep.tile([P, HALF], F32, name="picked_norms%d" % h, align_bytes=64) for h in range(2)]
        nc.vector.tensor_copy(picked_norms[0][:], norm_table[:].indirect(ncode_sb[:, lists[0]]))

        picked_scales = keep.tile([P, S], U8, name="picked_scales", align_bytes=64)
        nc.vector.tensor_copy(picked_scales[:], scale_table[:].indirect(offs_sb[:]))
        for r in range(4):
            nc.sync.dma_start(x_plane[r:P:32, :].bitcast(I32), picked_scales[8 * r : P : 32, :].bitcast(I32))

        w_grouped = shared.tile([P, TILES, QUADS, QUAD, PACK], BF16, name="w_grouped", offset=0, align_bytes=64)
        grouped = w_grouped[:].rearrange("p t a b j -> p a t b j")
        for h in range(2):
            nc.scalar.copy(
                grouped[:, h * QUADS // 2 : (h + 1) * QUADS // 2, :, :, :2],
                w_low[h][:].rearrange("p j (a t b) -> p a t b j", t=TILES, b=QUAD),
            )
            if h == 0:
                nc.scalar.activation(picked_norms[1][:], norm_table[:].indirect(ncode_sb[:, lists[1]]), ACT.Copy)
        high = w_high[:].rearrange("p j (a t b) -> p a t b j", t=TILES, b=QUAD)
        nc.scalar.copy(grouped[:, VECTOR_QUADS:, :, :, 2:], high[:, VECTOR_QUADS:])
        nc.vector.tensor_copy(grouped[:, :VECTOR_QUADS, :, :, 2:], high[:, :VECTOR_QUADS])

        row_norms = keep.tile([P, S], F32, name="row_norms", align_bytes=64)
        spread = shared.tile([P, S // P, RUNS, GROUP], F32, name="spread", offset=8192, align_bytes=64)
        for h in range(2):
            turned = psum.tile([P, 2, P], F32, name="turned", tag="bank%d_1" % (2 + h))
            for c in range(2):
                nc.tensor.transpose(turned[:, c, :], picked_norms[h][:, c * P : (c + 1) * P], identity[:])
            nc.scalar.copy(
                spread[:, 2 * h : 2 * h + 2],
                turned[:].rearrange("p c (r i) -> p c r i", r=RUNS)[:, :, :, 0:1].to_broadcast([P, 2, RUNS, GROUP]),
            )
        for h in range(2):
            turned_back = psum.tile([P, 2, P], F32, name="turned_back", tag="bank%d_0" % (2 + h))
            for c in range(2):
                nc.tensor.transpose(turned_back[:, c, :], spread[:, 2 * h + c].rearrange("p r i -> p (r i)"), identity[:])
            nc.scalar.copy(row_norms[:, halves[h]], turned_back[:].rearrange("p c j -> p (c j)"))

        w_codes = keep.tile([P, N], U32, name="w_codes", align_bytes=64)
        w_plane = keep.tile([P, N], U8, name="w_plane", align_bytes=64)
        nc.vector.quantize_mx(
            out=w_codes[:].bitcast(FP8X4),
            scales=w_plane[:],
            in_=w_grouped[:].rearrange("p t a b j -> p (t a b j)"),
        )

        picked_words = [
            shared.tile([P, HALF], U32, name="picked_words%d" % h, offset=4 * HALF * h, align_bytes=64) for h in range(2)
        ]
        for h in range(2):
            nc.vector.tensor_copy(picked_words[h][:], word_table[:].indirect(offs_sb[:, lists[h]]))

        neg = [keep.tile([P, S], F32, name="neg%d" % t, align_bytes=64) for t in range(TILES)]
        low = [shared.tile([P, 1], F32, name="low%d" % t, offset=4096 + 64 * (t % 2), align_bytes=64) for t in range(TILES)]
        exps = [keep.tile([P, S], F32, name="exps%d" % t, align_bytes=64) for t in range(TILES)]
        total = [keep.tile([P, 1], F32, name="total%d" % t) for t in range(TILES)]
        inverse = [keep.tile([P, 1], F32, name="inverse%d" % t) for t in range(TILES)]
        result = [keep.tile([P, S], F32, name="result%d" % t, align_bytes=64) for t in range(TILES)]
        out_rows = out.rearrange("(a t b) j -> t a b j", t=TILES, b=QUAD)

        def product(t, h):
            rows = slice(t * P, (t + 1) * P)
            bank = psum.tile([P, HALF], F32, name="bank", tag="bank%d_%d" % (t, h))
            nc.tensor.matmul_mx(
                out=bank[:],
                lhsT=w_codes[:, rows].bitcast(FP8X4),
                lhsT_scale=w_plane[:, rows],
                rhs=picked_words[h][:].bitcast(FP8X4),
                rhs_scale=x_plane[:, halves[h]],
                start=True,
                stop=True,
            )
            return bank

        def scores(t, h, bank):
            nc.vector.scalar_tensor_tensor(
                neg[t][:, halves[h]], bank[:], -1.0, row_norms[:, halves[h]], ALU.mult, ALU.mult
            )

        def scores_aside(t, h, bank):
            sums = keep.tile([P, HALF], F32, name="sums%d" % t, align_bytes=64)
            nc.scalar.activation(sums[:], bank[:], ACT.Copy, scale=-1.0)
            nc.gpsimd.tensor_tensor(neg[t][:, halves[h]], sums[:], row_norms[:, halves[h]], ALU.mult)

        def exponentials(t):
            nc.vector.tensor_reduce(low[t][:], neg[t][:], mybir.AxisListType.X, ALU.min)
            nc.scalar.activation(exps[t][:], neg[t][:], ACT.Exp, bias=low[t][:], scale=-1.0, accum_out=total[t][:])

        def invert(t):
            nc.vector.reciprocal(inverse[t][:], total[t][:])

        def normalise(t):
            if t == 0:
                nc.scalar.activation(result[t][:], exps[t][:], ACT.Copy, scale=inverse[t][:])
                nc.sync.dma_start(out_rows[t], result[t][:])
            elif t < TILES - 1:
                nc.vector.tensor_scalar(result[t][:], exps[t][:], inverse[t][:], None, ALU.mult)
                nc.sync.dma_start(out_rows[t], result[t][:])
            else:
                for cols, queue in zip(halves, (nc.sync, nc.scalar)):
                    nc.vector.tensor_scalar(result[t][:, cols], exps[t][:, cols], inverse[t][:], None, ALU.mult)
                    queue.dma_start(out_rows[t][:, :, cols], result[t][:, cols])

        for h in range(2):
            for t in range(2):
                scores(t, h, product(t, h))
        for t in range(2, TILES):
            scores_aside(t, 0, product(t, 0))
        banks = [product(t, 1) for t in range(2, TILES)]
        exponentials(0)
        exponentials(1)
        scores(2, 1, banks[0])
        scores(3, 1, banks[1])
        invert(0)
        normalise(0)
        exponentials(2)
        invert(1)
        exponentials(3)
        normalise(1)
        for t in range(2, TILES):
            invert(t)
            normalise(t)
